import numpy as np
import ml_dtypes


def mxq(x, axis, fmt="e4m3"):
    dtype, down = {"e4m3": (ml_dtypes.float8_e4m3fn, 7), "e5m2": (ml_dtypes.float8_e5m2, 14)}[fmt]
    v = np.moveaxis(np.asarray(x, np.float32).astype(ml_dtypes.bfloat16).astype(np.float64), axis, -1)
    blocks = v.reshape(v.shape[:-1] + (-1, 32))
    amax = np.abs(blocks).max(-1, keepdims=True)
    byte = np.maximum(np.where(amax > 0, np.frexp(amax)[1] - 1 + 127, 0) - down, 1)
    scale = np.exp2(byte - 127.0)
    codes = (blocks / scale).astype(np.float32).astype(dtype).astype(np.float64)
    return np.moveaxis((codes * scale).reshape(v.shape), -1, axis)


WIDE = False


def mx_kscale(k):
    if not WIDE:
        return np.ones(k)
    levels = np.array([10, -10, 5, -5, 0])
    if k % 512:
        return np.exp2(np.random.permutation(np.resize(levels, k // 32))).repeat(32)
    a = np.empty((k // 512, 16))
    for p in range(k // 512):
        a[p, :8] = np.random.permutation(np.resize(levels, 8))
        for g in range(8):
            far = levels[np.abs(levels - a[p, g]) >= 10]
            a[p, g + 8] = far[np.random.randint(len(far))]
    return np.exp2(a.ravel()).repeat(32)


def f64(x):
    return np.asarray(x).astype(np.float64)


def striped(idx):
    return np.tile(idx.reshape(-1, 16).T, (8, 1)).astype(np.uint16)


def unstriped(offs):
    return offs[:16].T.reshape(-1).astype(np.int64)


def striped8(idx):
    return np.concatenate([x.reshape(-1, 16).T for x in idx]).astype(np.uint16)


def runs(offs, k):
    lists = np.stack([offs[16 * r : 16 * r + 16].T.reshape(-1) for r in range(8)]).astype(np.int64)
    return lists[np.arange(k) % 512 // 64]


def pack_weight(w):
    k, n = w.shape
    w = f64(np.asarray(w, np.float32).astype(ml_dtypes.bfloat16)).reshape(k // 32, 32, n)
    amax = np.abs(w).max(1)
    byte = np.clip(np.where(amax > 0, np.frexp(amax)[1] - 1 + 127 - 7, 1), 1, 254)
    scaled = (w * np.exp2(127.0 - byte)[:, None, :]).reshape(k, n).astype(np.float32)
    words = np.ascontiguousarray(scaled.reshape(k // 512, 128, 4, n).transpose(0, 1, 3, 2)).astype(ml_dtypes.float8_e4m3fn).view(np.uint8)
    return words, np.ascontiguousarray(byte.astype(np.uint8).reshape(k // 512, 16, n))


def unpack_weight(words, scales):
    g, p, n, _ = words.shape
    vals = np.ascontiguousarray(words).view(ml_dtypes.float8_e4m3fn).astype(np.float64) * np.repeat(np.exp2(scales.astype(np.float64) - 127.0), 8, axis=1)[..., None]
    return vals.transpose(0, 1, 3, 2).reshape(g * 512, n)


def sigmoid(v):
    return 1.0 / (1.0 + np.exp(-np.maximum(v, -700.0)))


K, T, S, N, H = 512, 2048, 512, 512, 512


def setup_inputs():
    n = np.random.standard_normal
    s = mx_kscale(K)[:, None]
    u = mx_kscale(H)
    packed_xT = pack_weight(n((K, T)) * s)
    return {
        "x_words": packed_xT[0],
        "x_scales": packed_xT[1],
        "w1": (n((K, H)) / np.sqrt(K) / s).astype(np.float32),
        "gn": (np.random.uniform(0.5, 1.5, (H, 1)) * u[:, None]).astype(np.float32),
        "w2": (n((H, N)) / np.sqrt(H) / u[:, None]).astype(np.float32),
        "offs": striped(np.random.permutation(T)[:S]),
        "n1": striped8(np.stack([np.random.permutation(S) for _ in range(8)])),
        "n2": striped8(np.stack([np.random.permutation(S) for _ in range(8)])),
        "n3": striped8(np.stack([np.random.permutation(S) for _ in range(8)])),
    }


def reference(x_words, x_scales, w1, gn, w2, offs, n1, n2, n3):
    xq = unpack_weight(x_words, x_scales)[:, unstriped(offs)]
    y = mxq(f64(w1), 0, "e4m3").T @ xq
    z = f64(gn) * (y * (sigmoid(y[np.arange(H)[:, None], runs(n1, H)])))
    h = mxq(f64(w2), 0, "e4m3").T @ mxq(z, 0, "e4m3")
    return 0.75 * ((h - (h[np.arange(N)[:, None], runs(n2, N)])) * (h - (h[np.arange(N)[:, None], runs(n3, N)])))

@@ -1,0 +1,134 @@
+from contextlib import ExitStack
+
+import concourse.mybir as mybir
+
+K, T, S, H, N = 512, 2048, 512, 512, 512
+FLOPS = 2 * K * H * S + 2 * H * N * S
+
+F32 = mybir.dt.float32
+BF16 = mybir.dt.bfloat16
+I32 = mybir.dt.int32
+U32 = mybir.dt.uint32
+U16 = mybir.dt.uint16
+U8 = mybir.dt.uint8
+FP8X4 = mybir.dt.float8_e4m3fn_x4
+MULT = mybir.AluOpType.mult
+SUB = mybir.AluOpType.subtract
+SIGMOID = mybir.ActivationFunctionType.Sigmoid
+
+P = 128
+PACK = 4
+HALF = S // 2
+LIST_COLS = HALF // 16
+
+
+def tile_picked_laygatequad_none_p_kernel(tc, x_words, x_scales, w1, gn, w2, offs, n1, n2, n3, out):
+    nc = tc.nc
+    with ExitStack() as ctx:
+        keep = ctx.enter_context(tc.tile_pool(name="keep", bufs=1))
+        psum = ctx.enter_context(tc.psum_pool(name="psum", bufs=1))
+
+        def sb(shape, dtype, name):
+            return keep.tile(shape, dtype, name=name, align_bytes=64)
+
+        offs_t = sb([P, S // 16], U16, "offs_t")
+        n1_t = sb([P, S // 16], U16, "n1_t")
+        n2_t = sb([P, S // 16], U16, "n2_t")
+        n3_t = sb([P, S // 16], U16, "n3_t")
+
+        x_win = sb([P, T], U32, "x_win")
+        xs_win = sb([P, T], U8, "xs_win")
+        warm = sb([P, 1], F32, "warm")
+        warm_out = sb([P, 1], F32, "warm_out")
+        nc.vector.memset(xs_win[:].bitcast(I32), 0)
+        nc.vector.memset(warm[:], 0.0)
+        nc.scalar.activation(warm_out[:], warm[:], SIGMOID)
+
+        nc.sync.dma_start(offs_t[:], offs)
+        nc.sync.dma_start(x_win[:].bitcast(I32), x_words[0].rearrange("p n t -> p (n t)").bitcast(I32))
+        for q in range(4):
+            nc.sync.dma_start(xs_win[32 * q : 32 * q + 4, :].bitcast(I32), x_scales[0, 4 * q : 4 * q + 4, :].bitcast(I32))
+        w1_rows = w1.rearrange("(p j) c -> p j c", j=PACK)
+        w1_raw = []
+        for u in range(2):
+            raw = sb([P, PACK, H // 2], F32, "w1_raw%d" % u)
+            nc.sync.dma_start(raw[:], w1_rows[:, :, u * (H // 2) : (u + 1) * (H // 2)])
+            w1_raw.append(raw)
+        gn_t = sb([P, PACK], F32, "gn_t")
+        nc.sync.dma_start(n1_t[:], n1)
+        nc.sync.dma_start(gn_t[:], gn.rearrange("(p t) o -> p (t o)", t=PACK))
+        w2_raw = sb([P, PACK, N], F32, "w2_raw")
+        nc.sync.dma_start(w2_raw[:], w2.rearrange("(p j) c -> p j c", j=PACK))
+        nc.sync.dma_start(n2_t[:], n2)
+        nc.sync.dma_start(n3_t[:], n3)
+
+        x_codes = sb([P, S], U32, "x_codes")
+        x_bytes = sb([P, S], U8, "x_bytes")
+        nc.vector.tensor_copy(x_bytes[:], xs_win[:].indirect(offs_t[:]))
+        nc.vector.tensor_copy(x_codes[:], x_win[:].indirect(offs_t[:]))
+
+        w1_codes = sb([P, PACK, P], U32, "w1_codes")
+        w1_bytes = sb([P, PACK, P], U8, "w1_bytes")
+        for u in range(2):
+            dealt = sb([P, PACK, P // 2, PACK], BF16, "w1_dealt%d" % u)
+            dst = dealt[:].rearrange("p t m j -> p m j t")
+            src = w1_raw[u][:].rearrange("p j (m t) -> p m j t", t=PACK)
+            nc.vector.tensor_copy(dst[:, :44], src[:, :44])
+            nc.scalar.copy(dst[:, 44:], src[:, 44:])
+            cols = slice(u * (P // 2), (u + 1) * (P // 2))
+            for t in range(PACK):
+                nc.vector.quantize_mx(w1_codes[:, t, cols].bitcast(FP8X4), w1_bytes[:, t, cols], dealt[:, t].rearrange("p m j -> p (m j)"))
+
+        y_bank, y_win = [], []
+        for t in range(PACK):
+            bank = psum.tile([P, S], F32, name="y_bank%d" % t, tag="bank%d" % t)
+            nc.tensor.matmul_mx(bank[:], w1_codes[:, t, :].bitcast(FP8X4), w1_bytes[:, t, :], x_codes[:].bitcast(FP8X4), x_bytes[:], start=True, stop=True)
+            win = sb([P, S], F32, "y_win%d" % t)
+            if t % 2 == 0:
+                nc.scalar.copy(win[:], bank[:])
+            else:
+                nc.vector.tensor_copy(win[:], bank[:])
+            y_bank.append(bank)
+            y_win.append(win)
+
+        w2_dealt = sb([P, PACK, P, PACK], BF16, "w2_dealt")
+        w2_codes = sb([P, PACK, P], U32, "w2_codes")
+        w2_bytes = sb([P, PACK, P], U8, "w2_bytes")
+
+        h_win = [sb([P, S], F32, "h_win%d" % t) for t in range(PACK)]
+        h_row = [sb([P, S], F32, "h_row%d" % t) for t in range(PACK)]
+        for u in range(2):
+            cols = slice(u * HALF, (u + 1) * HALF)
+            lcols = slice(u * LIST_COLS, (u + 1) * LIST_COLS)
+            z_rows = sb([P, PACK, HALF], BF16, "z_rows%d" % u)
+            for t in range(PACK):
+                gate = sb([P, HALF], F32, "gate%d_%d" % (u, t))
+                nc.scalar.activation(gate[:], y_win[t][:].indirect(n1_t[:, lcols]), SIGMOID)
+                nc.vector.scalar_tensor_tensor(z_rows[:, t, :], y_bank[t][:, cols], gn_t[:, t : t + 1], gate[:], MULT, MULT)
+            z_woven = sb([P, HALF, PACK], BF16, "z_woven%d" % u)
+            nc.vector.tensor_copy(z_woven[:].rearrange("p (c i) t -> p c t i", i=4), z_rows[:].rearrange("p t (c i) -> p c t i", i=4))
+            if u == 0:
+                nc.vector.tensor_copy(w2_dealt[:].rearrange("p t m j -> p m j t"), w2_raw[:].rearrange("p j (m t) -> p m j t", t=PACK))
+            z_codes = sb([P, HALF], U32, "z_codes%d" % u)
+            z_bytes = sb([P, HALF], U8, "z_bytes%d" % u)
+            nc.vector.quantize_mx(z_codes[:].bitcast(FP8X4), z_bytes[:], z_woven[:].rearrange("p c t -> p (c t)"))
+            if u == 0:
+                nc.vector.quantize_mx(w2_codes[:].rearrange("p t m -> p (t m)").bitcast(FP8X4), w2_bytes[:].rearrange("p t m -> p (t m)"), w2_dealt[:].rearrange("p t m j -> p (t m j)"))
+            for t in range(PACK):
+                bank = psum.tile([P, HALF], F32, name="h_bank%d_%d" % (u, t), tag="bank%d" % (t + PACK * (1 - u)))
+                nc.tensor.matmul_mx(bank[:], w2_codes[:, t, :].bitcast(FP8X4), w2_bytes[:, t, :], z_codes[:].bitcast(FP8X4), z_bytes[:], start=True, stop=True)
+                nc.scalar.copy(h_win[t][:, cols], bank[:])
+                nc.scalar.copy(h_row[t][:, cols], bank[:])
+
+        out_rows = out.rearrange("(p t) j -> p t j", t=PACK)
+        for t in range(PACK):
+            for u in range(2):
+                cols = slice(u * HALF, (u + 1) * HALF)
+                lcols = slice(u * LIST_COLS, (u + 1) * LIST_COLS)
+                d2 = sb([P, HALF], F32, "d2_%d_%d" % (t, u))
+                d3 = sb([P, HALF], F32, "d3_%d_%d" % (t, u))
+                res = sb([P, HALF], F32, "res%d_%d" % (t, u))
+                nc.vector.tensor_tensor(d2[:], h_win[t][:].indirect(n2_t[:, lcols]), h_row[t][:, cols], SUB)
+                nc.vector.tensor_tensor(d3[:], h_win[t][:].indirect(n3_t[:, lcols]), h_row[t][:, cols], SUB)
+                nc.vector.scalar_tensor_tensor(res[:], d2[:], 0.75, d3[:], MULT, MULT)
+                nc.sync.dma_start(out_rows[:, t, cols], res[:])

@@ -15,11 +15,14 @@ FP8X4 = mybir.dt.float8_e4m3fn_x4
 MULT = mybir.AluOpType.mult
 SUB = mybir.AluOpType.subtract
 SIGMOID = mybir.ActivationFunctionType.Sigmoid
+COPY = mybir.ActivationFunctionType.Copy
 
 P = 128
 PACK = 4
 HALF = S // 2
-LIST_COLS = HALF // 16
+QUARTER = S // 4
+W1_PARTS = ((0, 64), (64, 128))
+Z_CHUNKS = ((0, 256), (256, 384), (384, 512))
 
 
 def tile_picked_laygatequad_none_p_kernel(tc, x_words, x_scales, w1, gn, w2, offs, n1, n2, n3, out):
@@ -28,8 +31,11 @@ def tile_picked_laygatequad_none_p_kernel(tc, x_words, x_scales, w1, gn, w2, off
         keep = ctx.enter_context(tc.tile_pool(name="keep", bufs=1))
         psum = ctx.enter_context(tc.psum_pool(name="psum", bufs=1))
 
-        def sb(shape, dtype, name):
-            return keep.tile(shape, dtype, name=name, align_bytes=64)
+        def sb(shape, dtype, name, tag=""):
+            return keep.tile(shape, dtype, name=name, tag=tag, align_bytes=64)
+
+        def entries(tile, lo, hi):
+            return tile[:, lo // 16 : hi // 16]
 
         offs_t = sb([P, S // 16], U16, "offs_t")
         n1_t = sb([P, S // 16], U16, "n1_t")
@@ -38,97 +44,164 @@ def tile_picked_laygatequad_none_p_kernel(tc, x_words, x_scales, w1, gn, w2, off
 
         x_win = sb([P, T], U32, "x_win")
         xs_win = sb([P, T], U8, "xs_win")
-        warm = sb([P, 1], F32, "warm")
-        warm_out = sb([P, 1], F32, "warm_out")
+        y_win = [sb([P, S], F32, "y_win%d" % t) for t in range(PACK)]
         nc.vector.memset(xs_win[:].bitcast(I32), 0)
-        nc.vector.memset(warm[:], 0.0)
-        nc.scalar.activation(warm_out[:], warm[:], SIGMOID)
 
+        w1_rows = w1.rearrange("(p j) c -> p j c", j=PACK)
+        w1_raw = [sb([P, PACK, PACK * (hi - lo)], F32, "w1_raw%d" % lo) for lo, hi in W1_PARTS]
+        w2_raw = sb([P, PACK, N], F32, "w2_raw")
+        gn_t = sb([P, PACK], F32, "gn_t")
         nc.sync.dma_start(offs_t[:], offs)
-        nc.sync.dma_start(x_win[:].bitcast(I32), x_words[0].rearrange("p n t -> p (n t)").bitcast(I32))
+        nc.sync.dma_start(w1_raw[0][:], w1_rows[:, :, : H // 2])
         for q in range(4):
             nc.sync.dma_start(xs_win[32 * q : 32 * q + 4, :].bitcast(I32), x_scales[0, 4 * q : 4 * q + 4, :].bitcast(I32))
-        w1_rows = w1.rearrange("(p j) c -> p j c", j=PACK)
-        w1_raw = []
-        for u in range(2):
-            raw = sb([P, PACK, H // 2], F32, "w1_raw%d" % u)
-            nc.sync.dma_start(raw[:], w1_rows[:, :, u * (H // 2) : (u + 1) * (H // 2)])
-            w1_raw.append(raw)
-        gn_t = sb([P, PACK], F32, "gn_t")
-        nc.sync.dma_start(n1_t[:], n1)
+        nc.sync.dma_start(x_win[:].bitcast(I32), x_words[0].rearrange("p n t -> p (n t)").bitcast(I32))
+        nc.sync.dma_start(w1_raw[1][:], w1_rows[:, :, H // 2 :])
         nc.sync.dma_start(gn_t[:], gn.rearrange("(p t) o -> p (t o)", t=PACK))
-        w2_raw = sb([P, PACK, N], F32, "w2_raw")
+        nc.sync.dma_start(n1_t[:], n1)
         nc.sync.dma_start(w2_raw[:], w2.rearrange("(p j) c -> p j c", j=PACK))
         nc.sync.dma_start(n2_t[:], n2)
         nc.sync.dma_start(n3_t[:], n3)
 
-        x_codes = sb([P, S], U32, "x_codes")
-        x_bytes = sb([P, S], U8, "x_bytes")
-        nc.vector.tensor_copy(x_bytes[:], xs_win[:].indirect(offs_t[:]))
-        nc.vector.tensor_copy(x_codes[:], x_win[:].indirect(offs_t[:]))
-
         w1_codes = sb([P, PACK, P], U32, "w1_codes")
         w1_bytes = sb([P, PACK, P], U8, "w1_bytes")
-        for u in range(2):
-            dealt = sb([P, PACK, P // 2, PACK], BF16, "w1_dealt%d" % u)
-            dst = dealt[:].rearrange("p t m j -> p m j t")
-            src = w1_raw[u][:].rearrange("p j (m t) -> p m j t", t=PACK)
-            nc.vector.tensor_copy(dst[:, :44], src[:, :44])
-            nc.scalar.copy(dst[:, 44:], src[:, 44:])
-            cols = slice(u * (P // 2), (u + 1) * (P // 2))
-            for t in range(PACK):
-                nc.vector.quantize_mx(w1_codes[:, t, cols].bitcast(FP8X4), w1_bytes[:, t, cols], dealt[:, t].rearrange("p m j -> p (m j)"))
+        w1_dealt = [sb([P, PACK, hi - lo, PACK], BF16, "w1_dealt%d" % lo) for lo, hi in W1_PARTS]
+        x_bytes = sb([P, S], U8, "x_bytes")
+        x_codes = sb([P, S], U32, "x_codes")
 
-        y_bank, y_win = [], []
+        def deal_w1(u, copy, tiles):
+            copy(w1_dealt[u][:].rearrange("p t m j -> p m j t")[:, :, :, tiles], w1_raw[u][:].rearrange("p j (m t) -> p m j t", t=PACK)[:, :, :, tiles])
+
+        def quantise_w1(u, tiles):
+            lo, hi = W1_PARTS[u]
+            for t in tiles:
+                nc.vector.quantize_mx(w1_codes[:, t, lo:hi].bitcast(FP8X4), w1_bytes[:, t, lo:hi], w1_dealt[u][:, t].rearrange("p m j -> p (m j)"))
+
+        deal_w1(0, nc.scalar.copy, slice(0, PACK))
+        nc.vector.tensor_copy(x_bytes[:], xs_win[:].indirect(offs_t[:]))
+        quantise_w1(0, range(PACK))
+        nc.vector.tensor_copy(x_codes[:], x_win[:].indirect(offs_t[:]))
+        deal_w1(1, nc.vector.tensor_copy, slice(0, 1))
+        quantise_w1(1, range(1))
+        deal_w1(1, nc.vector.tensor_copy, slice(1, PACK))
+        quantise_w1(1, range(1, PACK))
+
+        y_bank = []
         for t in range(PACK):
             bank = psum.tile([P, S], F32, name="y_bank%d" % t, tag="bank%d" % t)
             nc.tensor.matmul_mx(bank[:], w1_codes[:, t, :].bitcast(FP8X4), w1_bytes[:, t, :], x_codes[:].bitcast(FP8X4), x_bytes[:], start=True, stop=True)
-            win = sb([P, S], F32, "y_win%d" % t)
-            if t % 2 == 0:
-                nc.scalar.copy(win[:], bank[:])
-            else:
-                nc.vector.tensor_copy(win[:], bank[:])
             y_bank.append(bank)
-            y_win.append(win)
 
-        w2_dealt = sb([P, PACK, P, PACK], BF16, "w2_dealt")
-        w2_codes = sb([P, PACK, P], U32, "w2_codes")
-        w2_bytes = sb([P, PACK, P], U8, "w2_bytes")
+        w2_dealt = {}
+        w2_after = ("sig1_0", "z_last", "z_woven1", "z_woven2")
+        w2_codes = [sb([P, P], U32, "w2_codes%d" % t) for t in range(PACK)]
+        w2_bytes = [sb([P, P], U8, "w2_bytes%d" % t) for t in range(PACK)]
+        w2_cols = w2_raw[:].rearrange("p j (b t r) -> p t b r j", t=PACK, r=8)
 
-        h_win = [sb([P, S], F32, "h_win%d" % t) for t in range(PACK)]
-        h_row = [sb([P, S], F32, "h_row%d" % t) for t in range(PACK)]
-        for u in range(2):
-            cols = slice(u * HALF, (u + 1) * HALF)
-            lcols = slice(u * LIST_COLS, (u + 1) * LIST_COLS)
-            z_rows = sb([P, PACK, HALF], BF16, "z_rows%d" % u)
-            for t in range(PACK):
-                gate = sb([P, HALF], F32, "gate%d_%d" % (u, t))
-                nc.scalar.activation(gate[:], y_win[t][:].indirect(n1_t[:, lcols]), SIGMOID)
-                nc.vector.scalar_tensor_tensor(z_rows[:, t, :], y_bank[t][:, cols], gn_t[:, t : t + 1], gate[:], MULT, MULT)
-            z_woven = sb([P, HALF, PACK], BF16, "z_woven%d" % u)
-            nc.vector.tensor_copy(z_woven[:].rearrange("p (c i) t -> p c t i", i=4), z_rows[:].rearrange("p t (c i) -> p c t i", i=4))
-            if u == 0:
-                nc.vector.tensor_copy(w2_dealt[:].rearrange("p t m j -> p m j t"), w2_raw[:].rearrange("p j (m t) -> p m j t", t=PACK))
-            z_codes = sb([P, HALF], U32, "z_codes%d" % u)
-            z_bytes = sb([P, HALF], U8, "z_bytes%d" % u)
-            nc.vector.quantize_mx(z_codes[:].bitcast(FP8X4), z_bytes[:], z_woven[:].rearrange("p c t -> p (c t)"))
-            if u == 0:
-                nc.vector.quantize_mx(w2_codes[:].rearrange("p t m -> p (t m)").bitcast(FP8X4), w2_bytes[:].rearrange("p t m -> p (t m)"), w2_dealt[:].rearrange("p t m j -> p (t m j)"))
-            for t in range(PACK):
-                bank = psum.tile([P, HALF], F32, name="h_bank%d_%d" % (u, t), tag="bank%d" % (t + PACK * (1 - u)))
-                nc.tensor.matmul_mx(bank[:], w2_codes[:, t, :].bitcast(FP8X4), w2_bytes[:, t, :], z_codes[:].bitcast(FP8X4), z_bytes[:], start=True, stop=True)
-                nc.scalar.copy(h_win[t][:, cols], bank[:])
-                nc.scalar.copy(h_row[t][:, cols], bank[:])
+        def deal_w2(copy, t):
+            w2_dealt[t] = sb([P, P, PACK], BF16, "w2_dealt%d" % t, w2_after[t])
+            copy(w2_dealt[t][:].rearrange("p (b r) j -> p b r j", r=8), w2_cols[:, t])
 
-        out_rows = out.rearrange("(p t) j -> p t j", t=PACK)
-        for t in range(PACK):
-            for u in range(2):
-                cols = slice(u * HALF, (u + 1) * HALF)
-                lcols = slice(u * LIST_COLS, (u + 1) * LIST_COLS)
-                d2 = sb([P, HALF], F32, "d2_%d_%d" % (t, u))
-                d3 = sb([P, HALF], F32, "d3_%d_%d" % (t, u))
-                res = sb([P, HALF], F32, "res%d_%d" % (t, u))
-                nc.vector.tensor_tensor(d2[:], h_win[t][:].indirect(n2_t[:, lcols]), h_row[t][:, cols], SUB)
-                nc.vector.tensor_tensor(d3[:], h_win[t][:].indirect(n3_t[:, lcols]), h_row[t][:, cols], SUB)
-                nc.vector.scalar_tensor_tensor(res[:], d2[:], 0.75, d3[:], MULT, MULT)
-                nc.sync.dma_start(out_rows[:, t, cols], res[:])
+        def quantise_w2(t):
+            nc.vector.quantize_mx(w2_codes[t][:].bitcast(FP8X4), w2_bytes[t][:], w2_dealt[t][:].rearrange("p m j -> p (m j)"))
+
+        h_win = [sb([P, 2 * S if t in (1, 2) else S], F32, "h_win%d" % t) for t in range(PACK)]
+        h_row = [h_win[t + 1][:, S:] if t < 2 else sb([P, S], F32, "h_row%d" % t) for t in range(PACK)]
+        z_codes = sb([P, S], U32, "z_codes")
+        z_bytes = sb([P, S], U8, "z_bytes")
+        z_woven = {}
+        gained = sb([P, S], F32, "gained")
+        z_first = sb([P, PACK, HALF], F32, "z_first")
+        z_last = sb([P, 2, PACK, QUARTER], F32, "z_last", "z_last")
+
+        def z_at(t, lo, hi):
+            if lo < HALF:
+                return z_first[:, t, :].rearrange("p (q c) -> p q c", c=QUARTER)
+            return z_last[:, (lo - HALF) // QUARTER : (hi - HALF) // QUARTER, t, :]
+
+        def quarters(ap):
+            return ap.rearrange("p (q c) -> p q c", c=QUARTER)
+
+        def gate(t, lo, hi):
+            sig = sb([P, hi - lo], F32, "sig%d_%d" % (t, lo), "sig%d_%d" % (t, lo))
+            nc.scalar.activation(sig[:], y_win[t][:].indirect(entries(n1_t, lo, hi)), SIGMOID)
+            nc.vector.scalar_tensor_tensor(z_at(t, lo, hi), quarters(y_bank[t][:, lo:hi]), gn_t[:, t : t + 1], quarters(sig[:]), MULT, MULT)
+
+        def z_chunk(c):
+            return z_first[:] if c == 0 else z_last[:, c - 1]
+
+        def gate_first(c):
+            lo, hi = Z_CHUNKS[c]
+            nc.vector.tensor_tensor(z_chunk(c)[:, 0, :], y_win[0][:].indirect(entries(n1_t, lo, hi)), gained[:, lo:hi], MULT)
+
+        def weave(c, copy):
+            lo, hi = Z_CHUNKS[c]
+            z_woven[c] = sb([P, hi - lo, PACK], BF16, "z_woven%d" % c, "z_woven%d" % c)
+            copy(z_woven[c][:].rearrange("p (c i) t -> p c t i", i=4), z_chunk(c).rearrange("p t (c i) -> p c t i", i=4))
+
+        def quantise_z(c):
+            lo, hi = Z_CHUNKS[c]
+            nc.vector.quantize_mx(z_codes[:, lo:hi].bitcast(FP8X4), z_bytes[:, lo:hi], z_woven[c][:].rearrange("p c t -> p (c t)"))
+
+        def second_layer(t, lo, hi, bank_no, win_copy):
+            bank = psum.tile([P, hi - lo], F32, name="h_bank%d_%d" % (t, lo), tag="bank%d" % bank_no)
+            nc.tensor.matmul_mx(bank[:], w2_codes[t][:].bitcast(FP8X4), w2_bytes[t][:], z_codes[:, lo:hi].bitcast(FP8X4), z_bytes[:, lo:hi], start=True, stop=True)
+            win_copy(h_win[t][:, lo:hi], bank[:])
+            nc.scalar.copy(h_row[t][:, lo:hi], bank[:])
+
+        nc.scalar.activation(y_win[0][:], y_bank[0][:], SIGMOID)
+        nc.scalar.activation(gained[:], y_bank[0][:], COPY, scale=gn_t[:, 0:1])
+        nc.vector.tensor_copy(y_win[1][:], y_bank[1][:])
+        nc.vector.tensor_copy(y_win[2][:], y_bank[2][:])
+        gate_first(0)
+        gate(1, 0, HALF)
+        gate_first(1)
+        gate_first(2)
+        gate(2, 0, HALF)
+        nc.scalar.copy(y_win[3][:], y_bank[3][:])
+        deal_w2(nc.vector.tensor_copy, 0)
+        gate(3, 0, HALF)
+        quantise_w2(0)
+        weave(0, nc.vector.tensor_copy)
+        gate(1, HALF, S)
+        quantise_z(0)
+        gate(2, HALF, S)
+        gate(3, 256, 384)
+        gate(3, 384, 512)
+        weave(1, nc.scalar.copy)
+        weave(2, nc.vector.tensor_copy)
+        second_layer(0, 0, 256, 4, nc.scalar.copy)
+        quantise_z(2)
+        quantise_z(1)
+        deal_w2(nc.vector.tensor_copy, 1)
+        quantise_w2(1)
+        second_layer(0, 384, 512, 6, nc.scalar.copy)
+        second_layer(0, 256, 384, 5, nc.vector.tensor_copy)
+        second_layer(1, 0, S, 7, nc.scalar.copy)
+
+        out_rows = out.rearrange("(b t r) j -> t b r j", t=PACK, r=8)
+        pieces = [(t, lo, hi) for t in range(PACK) for lo, hi in (((0, HALF), (HALF, S)), ((0, S),), ((0, S),), Z_CHUNKS)[t]]
+        diffs = {}
+
+        def differ(i, which, table):
+            t, lo, hi = pieces[i]
+            diffs[i, which] = sb([P, hi - lo], F32, "d%d_%d" % (which, i), "d%d_%d" % (which, i))
+            nc.vector.tensor_tensor(diffs[i, which][:], h_win[t][:].indirect(entries(table, lo, hi)), h_row[t][:, lo:hi], SUB)
+
+        def finish(i):
+            t, lo, hi = pieces[i]
+            res = sb([P, hi - lo], F32, "res%d" % i)
+            nc.vector.scalar_tensor_tensor(res[:], diffs[i, 2][:], 0.75, diffs[i, 3][:], MULT, MULT)
+            nc.sync.dma_start(out_rows[t][:, :, lo:hi], res[:])
+
+        for i in range(len(pieces)):
+            differ(i, 2, n2_t)
+            if i > 0:
+                finish(i - 1)
+            differ(i, 3, n3_t)
+            if i in (0, 1):
+                t = 2 + i
+                deal_w2(nc.scalar.copy, t)
+                quantise_w2(t)
+                second_layer(t, 0, S, t, nc.scalar.copy)
+        finish(len(pieces) - 1)

@@ -69,22 +69,21 @@ def tile_picked_laygatequad_none_p_kernel(tc, x_words, x_scales, w1, gn, w2, off
         x_bytes = sb([P, S], U8, "x_bytes")
         x_codes = sb([P, S], U32, "x_codes")
 
-        def deal_w1(u, copy, tiles):
-            copy(w1_dealt[u][:].rearrange("p t m j -> p m j t")[:, :, :, tiles], w1_raw[u][:].rearrange("p j (m t) -> p m j t", t=PACK)[:, :, :, tiles])
+        def deal_w1(u, copy, lo, hi):
+            copy(w1_dealt[u][:].rearrange("p t m j -> p m j t")[:, lo:hi], w1_raw[u][:].rearrange("p j (m t) -> p m j t", t=PACK)[:, lo:hi])
 
-        def quantise_w1(u, tiles):
+        def quantise_w1(u):
             lo, hi = W1_PARTS[u]
-            for t in tiles:
+            for t in range(PACK):
                 nc.vector.quantize_mx(w1_codes[:, t, lo:hi].bitcast(FP8X4), w1_bytes[:, t, lo:hi], w1_dealt[u][:, t].rearrange("p m j -> p (m j)"))
 
-        deal_w1(0, nc.scalar.copy, slice(0, PACK))
+        deal_w1(0, nc.vector.tensor_copy, 0, P // 2)
         nc.vector.tensor_copy(x_bytes[:], xs_win[:].indirect(offs_t[:]))
-        quantise_w1(0, range(PACK))
+        quantise_w1(0)
         nc.vector.tensor_copy(x_codes[:], x_win[:].indirect(offs_t[:]))
-        deal_w1(1, nc.vector.tensor_copy, slice(0, 1))
-        quantise_w1(1, range(1))
-        deal_w1(1, nc.vector.tensor_copy, slice(1, PACK))
-        quantise_w1(1, range(1, PACK))
+        deal_w1(1, nc.vector.tensor_copy, 0, 40)
+        deal_w1(1, nc.scalar.copy, 40, P // 2)
+        quantise_w1(1)
 
         y_bank = []
         for t in range(PACK):
@@ -93,7 +92,7 @@ def tile_picked_laygatequad_none_p_kernel(tc, x_words, x_scales, w1, gn, w2, off
             y_bank.append(bank)
 
         w2_dealt = {}
-        w2_after = ("sig1_0", "z_last", "z_woven1", "z_woven2")
+        w2_after = ("sig1_0", "z_last", "sig3_384", "z_woven2")
         w2_codes = [sb([P, P], U32, "w2_codes%d" % t) for t in range(PACK)]
         w2_bytes = [sb([P, P], U8, "w2_bytes%d" % t) for t in range(PACK)]
         w2_cols = w2_raw[:].rearrange("p j (b t r) -> p t b r j", t=PACK, r=8)
@@ -134,10 +133,10 @@ def tile_picked_laygatequad_none_p_kernel(tc, x_words, x_scales, w1, gn, w2, off
             lo, hi = Z_CHUNKS[c]
             nc.vector.tensor_tensor(z_chunk(c)[:, 0, :], y_win[0][:].indirect(entries(n1_t, lo, hi)), gained[:, lo:hi], MULT)
 
-        def weave(c, copy):
+        def weave(c):
             lo, hi = Z_CHUNKS[c]
             z_woven[c] = sb([P, hi - lo, PACK], BF16, "z_woven%d" % c, "z_woven%d" % c)
-            copy(z_woven[c][:].rearrange("p (c i) t -> p c t i", i=4), z_chunk(c).rearrange("p t (c i) -> p c t i", i=4))
+            nc.vector.tensor_copy(z_woven[c][:].rearrange("p (c i) t -> p c t i", i=4), z_chunk(c).rearrange("p t (c i) -> p c t i", i=4))
 
         def quantise_z(c):
             lo, hi = Z_CHUNKS[c]
@@ -162,21 +161,21 @@ def tile_picked_laygatequad_none_p_kernel(tc, x_words, x_scales, w1, gn, w2, off
         deal_w2(nc.vector.tensor_copy, 0)
         gate(3, 0, HALF)
         quantise_w2(0)
-        weave(0, nc.vector.tensor_copy)
+        weave(0)
         gate(1, HALF, S)
-        quantise_z(0)
         gate(2, HALF, S)
+        quantise_z(0)
         gate(3, 256, 384)
         gate(3, 384, 512)
-        weave(1, nc.scalar.copy)
-        weave(2, nc.vector.tensor_copy)
-        second_layer(0, 0, 256, 4, nc.scalar.copy)
-        quantise_z(2)
+        weave(1)
+        weave(2)
         quantise_z(1)
+        second_layer(0, 0, 256, 4, nc.scalar.copy)
+        second_layer(0, 256, 384, 5, nc.scalar.copy)
+        quantise_z(2)
         deal_w2(nc.vector.tensor_copy, 1)
         quantise_w2(1)
-        second_layer(0, 384, 512, 6, nc.scalar.copy)
-        second_layer(0, 256, 384, 5, nc.vector.tensor_copy)
+        second_layer(0, 384, 512, 6, nc.vector.tensor_copy)
         second_layer(1, 0, S, 7, nc.scalar.copy)
 
         out_rows = out.rearrange("(b t r) j -> t b r j", t=PACK, r=8)

@@ -77,7 +77,7 @@ def tile_picked_laygatequad_none_p_kernel(tc, x_words, x_scales, w1, gn, w2, off
             for t in range(PACK):
                 nc.vector.quantize_mx(w1_codes[:, t, lo:hi].bitcast(FP8X4), w1_bytes[:, t, lo:hi], w1_dealt[u][:, t].rearrange("p m j -> p (m j)"))
 
-        deal_w1(0, nc.vector.tensor_copy, 0, P // 2)
+        deal_w1(0, nc.scalar.copy, 0, P // 2)
         nc.vector.tensor_copy(x_bytes[:], xs_win[:].indirect(offs_t[:]))
         quantise_w1(0)
         nc.vector.tensor_copy(x_codes[:], x_win[:].indirect(offs_t[:]))

from contextlib import ExitStack

import concourse.mybir as mybir

K, T, S, H, N = 512, 2048, 512, 512, 512
FLOPS = 2 * K * H * S + 2 * H * N * S

F32 = mybir.dt.float32
BF16 = mybir.dt.bfloat16
I32 = mybir.dt.int32
U32 = mybir.dt.uint32
U16 = mybir.dt.uint16
U8 = mybir.dt.uint8
FP8X4 = mybir.dt.float8_e4m3fn_x4
MULT = mybir.AluOpType.mult
SUB = mybir.AluOpType.subtract
SIGMOID = mybir.ActivationFunctionType.Sigmoid
COPY = mybir.ActivationFunctionType.Copy

P = 128
PACK = 4
HALF = S // 2
QUARTER = S // 4
W1_PARTS = ((0, 64), (64, 128))
Z_CHUNKS = ((0, 256), (256, 384), (384, 512))


def tile_picked_laygatequad_none_p_kernel(tc, x_words, x_scales, w1, gn, w2, offs, n1, n2, n3, out):
    nc = tc.nc
    with ExitStack() as ctx:
        keep = ctx.enter_context(tc.tile_pool(name="keep", bufs=1))
        psum = ctx.enter_context(tc.psum_pool(name="psum", bufs=1))

        def sb(shape, dtype, name, tag=""):
            return keep.tile(shape, dtype, name=name, tag=tag, align_bytes=64)

        def entries(tile, lo, hi):
            return tile[:, lo // 16 : hi // 16]

        offs_t = sb([P, S // 16], U16, "offs_t")
        n1_t = sb([P, S // 16], U16, "n1_t")
        n2_t = sb([P, S // 16], U16, "n2_t")
        n3_t = sb([P, S // 16], U16, "n3_t")

        x_win = sb([P, T], U32, "x_win")
        xs_win = sb([P, T], U8, "xs_win")
        y_win = [sb([P, S], F32, "y_win%d" % t) for t in range(PACK)]
        nc.vector.memset(xs_win[:].bitcast(I32), 0)

        w1_rows = w1.rearrange("(p j) c -> p j c", j=PACK)
        w1_raw = [sb([P, PACK, PACK * (hi - lo)], F32, "w1_raw%d" % lo) for lo, hi in W1_PARTS]
        w2_raw = sb([P, PACK, N], F32, "w2_raw")
        gn_t = sb([P, PACK], F32, "gn_t")
        nc.sync.dma_start(offs_t[:], offs)
        nc.sync.dma_start(w1_raw[0][:], w1_rows[:, :, : H // 2])
        for q in range(4):
            nc.sync.dma_start(xs_win[32 * q : 32 * q + 4, :].bitcast(I32), x_scales[0, 4 * q : 4 * q + 4, :].bitcast(I32))
        nc.sync.dma_start(x_win[:].bitcast(I32), x_words[0].rearrange("p n t -> p (n t)").bitcast(I32))
        nc.sync.dma_start(w1_raw[1][:], w1_rows[:, :, H // 2 :])
        nc.sync.dma_start(gn_t[:], gn.rearrange("(p t) o -> p (t o)", t=PACK))
        nc.sync.dma_start(n1_t[:], n1)
        nc.sync.dma_start(w2_raw[:], w2.rearrange("(p j) c -> p j c", j=PACK))
        nc.sync.dma_start(n2_t[:], n2)
        nc.sync.dma_start(n3_t[:], n3)

        w1_codes = sb([P, PACK, P], U32, "w1_codes")
        w1_bytes = sb([P, PACK, P], U8, "w1_bytes")
        w1_dealt = [sb([P, PACK, hi - lo, PACK], BF16, "w1_dealt%d" % lo) for lo, hi in W1_PARTS]
        x_bytes = sb([P, S], U8, "x_bytes")
        x_codes = sb([P, S], U32, "x_codes")

        def deal_w1(u, copy, lo, hi):
            copy(w1_dealt[u][:].rearrange("p t m j -> p m j t")[:, lo:hi], w1_raw[u][:].rearrange("p j (m t) -> p m j t", t=PACK)[:, lo:hi])

        def quantise_w1(u):
            lo, hi = W1_PARTS[u]
            for t in range(PACK):
                nc.vector.quantize_mx(w1_codes[:, t, lo:hi].bitcast(FP8X4), w1_bytes[:, t, lo:hi], w1_dealt[u][:, t].rearrange("p m j -> p (m j)"))

        deal_w1(0, nc.scalar.copy, 0, P // 2)
        nc.vector.tensor_copy(x_bytes[:], xs_win[:].indirect(offs_t[:]))
        quantise_w1(0)
        nc.vector.tensor_copy(x_codes[:], x_win[:].indirect(offs_t[:]))
        deal_w1(1, nc.vector.tensor_copy, 0, 40)
        deal_w1(1, nc.scalar.copy, 40, P // 2)
        quantise_w1(1)

        y_bank = []
        for t in range(PACK):
            bank = psum.tile([P, S], F32, name="y_bank%d" % t, tag="bank%d" % t)
            nc.tensor.matmul_mx(bank[:], w1_codes[:, t, :].bitcast(FP8X4), w1_bytes[:, t, :], x_codes[:].bitcast(FP8X4), x_bytes[:], start=True, stop=True)
            y_bank.append(bank)

        w2_dealt = {}
        w2_after = ("sig1_0", "z_last", "sig3_384", "z_woven2")
        w2_codes = [sb([P, P], U32, "w2_codes%d" % t) for t in range(PACK)]
        w2_bytes = [sb([P, P], U8, "w2_bytes%d" % t) for t in range(PACK)]
        w2_cols = w2_raw[:].rearrange("p j (b t r) -> p t b r j", t=PACK, r=8)

        def deal_w2(copy, t):
            w2_dealt[t] = sb([P, P, PACK], BF16, "w2_dealt%d" % t, w2_after[t])
            copy(w2_dealt[t][:].rearrange("p (b r) j -> p b r j", r=8), w2_cols[:, t])

        def quantise_w2(t):
            nc.vector.quantize_mx(w2_codes[t][:].bitcast(FP8X4), w2_bytes[t][:], w2_dealt[t][:].rearrange("p m j -> p (m j)"))

        h_win = [sb([P, 2 * S if t in (1, 2) else S], F32, "h_win%d" % t) for t in range(PACK)]
        h_row = [h_win[t + 1][:, S:] if t < 2 else sb([P, S], F32, "h_row%d" % t) for t in range(PACK)]
        z_codes = sb([P, S], U32, "z_codes")
        z_bytes = sb([P, S], U8, "z_bytes")
        z_woven = {}
        gained = sb([P, S], F32, "gained")
        z_first = sb([P, PACK, HALF], F32, "z_first")
        z_last = sb([P, 2, PACK, QUARTER], F32, "z_last", "z_last")

        def z_at(t, lo, hi):
            if lo < HALF:
                return z_first[:, t, :].rearrange("p (q c) -> p q c", c=QUARTER)
            return z_last[:, (lo - HALF) // QUARTER : (hi - HALF) // QUARTER, t, :]

        def quarters(ap):
            return ap.rearrange("p (q c) -> p q c", c=QUARTER)

        def gate(t, lo, hi):
            sig = sb([P, hi - lo], F32, "sig%d_%d" % (t, lo), "sig%d_%d" % (t, lo))
            nc.scalar.activation(sig[:], y_win[t][:].indirect(entries(n1_t, lo, hi)), SIGMOID)
            nc.vector.scalar_tensor_tensor(z_at(t, lo, hi), quarters(y_bank[t][:, lo:hi]), gn_t[:, t : t + 1], quarters(sig[:]), MULT, MULT)

        def z_chunk(c):
            return z_first[:] if c == 0 else z_last[:, c - 1]

        def gate_first(c):
            lo, hi = Z_CHUNKS[c]
            nc.vector.tensor_tensor(z_chunk(c)[:, 0, :], y_win[0][:].indirect(entries(n1_t, lo, hi)), gained[:, lo:hi], MULT)

        def weave(c):
            lo, hi = Z_CHUNKS[c]
            z_woven[c] = sb([P, hi - lo, PACK], BF16, "z_woven%d" % c, "z_woven%d" % c)
            nc.vector.tensor_copy(z_woven[c][:].rearrange("p (c i) t -> p c t i", i=4), z_chunk(c).rearrange("p t (c i) -> p c t i", i=4))

        def quantise_z(c):
            lo, hi = Z_CHUNKS[c]
            nc.vector.quantize_mx(z_codes[:, lo:hi].bitcast(FP8X4), z_bytes[:, lo:hi], z_woven[c][:].rearrange("p c t -> p (c t)"))

        def second_layer(t, lo, hi, bank_no, win_copy):
            bank = psum.tile([P, hi - lo], F32, name="h_bank%d_%d" % (t, lo), tag="bank%d" % bank_no)
            nc.tensor.matmul_mx(bank[:], w2_codes[t][:].bitcast(FP8X4), w2_bytes[t][:], z_codes[:, lo:hi].bitcast(FP8X4), z_bytes[:, lo:hi], start=True, stop=True)
            win_copy(h_win[t][:, lo:hi], bank[:])
            nc.scalar.copy(h_row[t][:, lo:hi], bank[:])

        nc.scalar.activation(y_win[0][:], y_bank[0][:], SIGMOID)
        nc.scalar.activation(gained[:], y_bank[0][:], COPY, scale=gn_t[:, 0:1])
        nc.vector.tensor_copy(y_win[1][:], y_bank[1][:])
        nc.vector.tensor_copy(y_win[2][:], y_bank[2][:])
        gate_first(0)
        gate(1, 0, HALF)
        gate_first(1)
        gate_first(2)
        gate(2, 0, HALF)
        nc.scalar.copy(y_win[3][:], y_bank[3][:])
        deal_w2(nc.vector.tensor_copy, 0)
        gate(3, 0, HALF)
        quantise_w2(0)
        weave(0)
        gate(1, HALF, S)
        gate(2, HALF, S)
        quantise_z(0)
        gate(3, 256, 384)
        gate(3, 384, 512)
        weave(1)
        weave(2)
        quantise_z(1)
        second_layer(0, 0, 256, 4, nc.scalar.copy)
        second_layer(0, 256, 384, 5, nc.scalar.copy)
        quantise_z(2)
        deal_w2(nc.vector.tensor_copy, 1)
        quantise_w2(1)
        second_layer(0, 384, 512, 6, nc.vector.tensor_copy)
        second_layer(1, 0, S, 7, nc.scalar.copy)

        out_rows = out.rearrange("(b t r) j -> t b r j", t=PACK, r=8)
        pieces = [(t, lo, hi) for t in range(PACK) for lo, hi in (((0, HALF), (HALF, S)), ((0, S),), ((0, S),), Z_CHUNKS)[t]]
        diffs = {}

        def differ(i, which, table):
            t, lo, hi = pieces[i]
            diffs[i, which] = sb([P, hi - lo], F32, "d%d_%d" % (which, i), "d%d_%d" % (which, i))
            nc.vector.tensor_tensor(diffs[i, which][:], h_win[t][:].indirect(entries(table, lo, hi)), h_row[t][:, lo:hi], SUB)

        def finish(i):
            t, lo, hi = pieces[i]
            res = sb([P, hi - lo], F32, "res%d" % i)
            nc.vector.scalar_tensor_tensor(res[:], diffs[i, 2][:], 0.75, diffs[i, 3][:], MULT, MULT)
            nc.sync.dma_start(out_rows[t][:, :, lo:hi], res[:])

        for i in range(len(pieces)):
            differ(i, 2, n2_t)
            if i > 0:
                finish(i - 1)
            differ(i, 3, n3_t)
            if i in (0, 1):
                t = 2 + i
                deal_w2(nc.scalar.copy, t)
                quantise_w2(t)
                second_layer(t, 0, S, t, nc.scalar.copy)
        finish(len(pieces) - 1)
